import numpy as np, ml_dtypes
CORES = [24,25,26,27,28,29,30,31,224,225,226,227,228,229,230,231]
N = 16
VB, TK = 1, 512
def setup_inputs(rng):
    h = (rng.standard_normal((128, TK), dtype=np.float32) / 8).astype(ml_dtypes.bfloat16)
    return {"h": np.broadcast_to(h, (N, 128, TK)).copy(), "w": rng.standard_normal((N, 128, VB * 128), dtype=np.float32).astype(ml_dtypes.bfloat16)}
def setup_inputs_big(rng):
    d = setup_inputs(rng)
    for k in ("h", "w"): d[k] = (d[k].astype(np.float32) * 1024.0).astype(d[k].dtype)
    return d
def setup_inputs_small(rng):
    d = setup_inputs(rng)
    for k in ("h", "w"): d[k] = (d[k].astype(np.float32) * (1 / 1024.0)).astype(d[k].dtype)
    return d
def setup_inputs_apart(rng):
    d = setup_inputs(rng)
    f = (10.0 ** rng.permutation(np.linspace(-1.5, 1.5, N))).astype(np.float32).reshape(N, 1, 1)
    for k in ("w",): d[k] = (d[k].astype(np.float32) * f).astype(d[k].dtype)
    return d
def setup_inputs_neg(rng):
    d = setup_inputs(rng)
    d["h"] = (np.abs(d["h"].astype(np.float32)) * 1048576.0).astype(d["h"].dtype); d["w"] = (-np.abs(d["w"].astype(np.float32))).astype(d["w"].dtype)
    return d
def reference(h, w):
    H, W = h.astype(np.float64), w.astype(np.float64)
    Z = np.concatenate([W[r].T @ H[r] for r in range(N)], axis=0)
    m = Z.max(axis=0)
    s = np.maximum(Z - 0.5 * m, 0.0).sum(axis=0)
    return {"m": np.broadcast_to(m.astype(np.float32), (N, 1, TK)), "s": np.broadcast_to(s.astype(np.float32), (N, 1, TK))}

@@ -1,0 +1,241 @@
+from concourse.bass import DstId, RemoteDMATransfer
+from concourse.mybir import AluOpType
+
+F, B = "float32", "bfloat16"
+SCRATCH = {
+    "h_sb": ("sbuf", [128, 512], B), "hp": ("sbuf", [128, 512], B),
+    "w_sb": ("sbuf", [128, 128], B), "wn_sb": ("sbuf", [128, 128], B), "wp_sb": ("sbuf", [128, 128], B),
+    "E": ("sbuf", [128, 129], B), "Dd": ("dram", [129, 128], B), "I_bf": ("sbuf", [128, 128], B),
+    "negh": ("sbuf", [128, 512], B), "csp": ("sbuf", [128, 128], B), "cT": ("sbuf", [128, 128], B),
+    "zero": ("sbuf", [128, 256], F), "ones": ("sbuf", [128, 4], F),
+    "zodd": ("sbuf", [128, 256], F), "S1": ("sbuf", [128, 128], F), "S2": ("sbuf", [128, 64], F),
+    "S3": ("sbuf", [128, 64], F), "S4": ("sbuf", [128, 32], F), "S5": ("sbuf", [128, 16], F), "S6": ("sbuf", [128, 8], F),
+    "land_m": ("sbuf", [128, 32], F), "G1": ("sbuf", [128, 16], F), "G2": ("sbuf", [128, 8], F),
+    "cm_own": ("sbuf", [128, 4], F), "cm_rem": ("sbuf", [128, 4], F), "m4": ("sbuf", [128, 4], F), "r1": ("sbuf", [128, 4], F),
+    "RA": ("sbuf", [128, 512], F), "RB": ("sbuf", [128, 512], F), "SA": ("sbuf", [128, 4], F),
+    "land_s": ("sbuf", [128, 32], F), "A1": ("sbuf", [128, 16], F), "A2": ("sbuf", [128, 8], F), "s4": ("sbuf", [128, 4], F),
+    "zT": ("psum", [128, 512], F), "P": ("psum", [128, 512], F), "cTp": ("psum", [128, 512], F), "Sp": ("psum", [128, 512], F),
+    "ZA0": ("psum", [128, 512], F), "ZA1": ("psum", [128, 512], F), "ZB0": ("psum", [128, 512], F), "ZB1": ("psum", [128, 512], F),
+}
+SEMAPHORES = ["lh", "lw", "idm", "v", "pz", "pT", "pA0", "pA1", "pB0", "pB1", "psA", "psB",
+              "wn", "wp", "ma", "cmo", "cmr", "sa", "snt", "stm", "sts"]
+
+
+def _bits(mask):
+    return bin(mask).count("1")
+
+
+def _plan(topo, here, there):
+    owners = [c for c in here if topo.may_write(c, there[0])]
+    owner_of, partner = {}, {}
+    for d in sorted(set(topo.die(c) for c in here)):
+        od = [c for c in owners if topo.die(c) == d]
+        nd = [c for c in here if topo.die(c) == d and c not in owners]
+        for k, c in enumerate(nd):
+            owner_of[c] = od[k % len(od)]
+        hd = [c for c in here if topo.die(c) == d]
+        td = [c for c in there if topo.die(c) == d]
+        for k, c in enumerate(hd):
+            partner[c] = td[k]
+    return owners, owner_of, partner
+
+
+def rank_program(g, core, T, topo):
+    if T.rank_of(core) is None:
+        return
+    S, V, PE = T.sem, g.vector, g.tensor
+    MAX, ADD, SUB = AluOpType.max, AluOpType.add, AluOpType.subtract
+    cores = list(T.cores)
+    mine = [c for c in cores if (topo.host(c), topo.chip(c)) == (topo.host(core), topo.chip(core))]
+    other = [c for c in cores if c not in mine]
+    owners, owner_of, partner = _plan(topo, mine, other)
+    owners_o, owner_of_o, partner_o = _plan(topo, other, mine)
+    is_owner = core in owners
+    slot = mine.index(core)
+    my_slot = slice(4 * slot, 4 * slot + 4)
+    wsrc = [c for c in other if partner_o[c] == core][0]
+    early = wsrc in owners_o
+    wfrom = wsrc if early else owner_of_o[wsrc]
+    n_far = _bits(topo.mask(wfrom, core))
+    peers = [c for c in mine if c != core]
+    m_on = topo.mask(core, peers[0])
+
+    def did(d):
+        rid, pid = topo.addr(d, core)
+        return DstId(rid=rid, pnc=pid)
+
+    nv = [0]
+
+    def vop(ins):
+        ins.then_inc(S.v, 1)
+        nv[0] += 1
+        V.wait_ge(S.v, nv[0])
+        return nv[0]
+
+    g.sync.dma_start(T.h_sb[:, :], T.h[:, :]).then_inc(S.lh, 16)
+    g.scalar.dma_start(T.w_sb[:, :], T.w[:, :]).then_inc(S.lw, 16)
+
+    vop(V.memset(T.E[:, :], 0.0))
+    n_E = vop(V.memset(T.E[:, 0:1], 1.0))
+    vop(V.memset(T.csp[:, :], 0.0))
+    vop(V.memset(T.negh[:, :], 0.0))
+    for b in range(4):
+        vop(V.memset(T.negh[32 * b:32 * b + 32, 128 * b:128 * b + 128], -0.5))
+    vop(V.memset(T.ones[:, :], 1.0))
+    vop(V.memset(T.zero[:, :], 0.0))
+    g.sync.wait_ge(S.v, n_E)
+    g.sync.dma_start(T.Dd[:, :], T.E[:, :]).then_inc(S.idm, 16)
+    g.sync.wait_ge(S.idm, 16)
+    g.sync.dma_start(T.I_bf[:, :], T.Dd[0:128, :]).then_inc(S.idm, 16)
+
+    PE.wait_ge(S.lh, 16)
+    PE.wait_ge(S.lw, 16)
+    for b in range(4):
+        PE.matmul(T.zT[:, 128 * b:128 * b + 128], T.h_sb[:, b:512:4], T.w_sb[:, :], True, True).then_inc(S.pz, 1)
+    V.wait_ge(S.pz, 4)
+    vop(V.tensor_copy(T.zodd[:, :], T.zT[:, 1:512:2]))
+    vop(V.tensor_tensor(T.P[:, 0:128], T.zT[:, 0:512:4], T.zodd[:, 0:256:2], MAX))
+    vop(V.tensor_tensor(T.S1[:, :], T.zT[:, 2:512:4], T.zodd[:, 1:256:2], MAX))
+    vop(V.tensor_tensor(T.P[:, 128:192], T.P[:, 0:128:2], T.S1[:, 0:128:2], MAX))
+    vop(V.tensor_tensor(T.S2[:, :], T.P[:, 1:128:2], T.S1[:, 1:128:2], MAX))
+    vop(V.tensor_tensor(T.S3[:, :], T.P[:, 128:192], T.S2[:, :], MAX))
+    vop(V.tensor_tensor(T.S4[:, :], T.S3[:, 0:64:2], T.S3[:, 1:64:2], MAX))
+    vop(V.tensor_tensor(T.S5[:, :], T.S4[:, 0:32:2], T.S4[:, 1:32:2], MAX))
+    vop(V.tensor_tensor(T.S6[:, :], T.S5[:, 0:16:2], T.S5[:, 1:16:2], MAX))
+    n_piece = vop(V.tensor_tensor(T.land_m[:, my_slot], T.S6[:, 0:8:2], T.S6[:, 1:8:2], MAX))
+
+    for b in range(4):
+        n_hp = vop(V.tensor_copy(T.hp[:, 128 * b:128 * b + 128], T.h_sb[:, b:512:4]))
+    PE.wait_ge(S.v, n_hp)
+    PE.matmul(T.ZA0[:, 0:256], T.w_sb[:, :], T.hp[:, 0:256], True, False)
+    PE.matmul(T.ZA1[:, 0:256], T.w_sb[:, :], T.hp[:, 256:512], True, False)
+
+    def scores_b():
+        PE.wait_ge(S.wp, n_far)
+        PE.matmul(T.ZB0[:, 0:256], T.wp_sb[:, :], T.hp[:, 0:256], True, False)
+        PE.matmul(T.ZB1[:, 0:256], T.wp_sb[:, :], T.hp[:, 256:512], True, False)
+
+    if early:
+        scores_b()
+
+    sent = 0
+    all_slots = [T.land_m[:, 4 * k:4 * k + 4] for k in range(len(mine))]
+    g.wait_ge(S.lw, 16)
+    if is_owner:
+        nb = [c for c in mine if owner_of.get(c) == core]
+        m_off = topo.mask(core, partner[core])
+        m_rest = m_on & ~m_off
+        n_ma = sum(_bits(topo.mask(c, core) & (topo.mask(c, partner[c]) if c in owners else topo.mask(c, core)))
+                   for c in peers)
+        rid, pid = topo.addr(partner[core], core)
+        g.remote_dma(out_ap=T.wp_sb[:, :], in_ap=T.w_sb[:, :], remote_sem=S.wp, local_sem=S.snt, pid=pid, routing_id=rid,
+                     dma_engine_mask=m_off)
+        sent += _bits(m_off)
+        g.wait_ge(S.v, n_piece)
+        to = [c for c in owners if c != core]
+        g.remote_dma_fused([RemoteDMATransfer(dst_ids=[did(c) for c in to], dma_engine_mask=m_off, remote_sem=S.ma,
+                                              srcs=[T.land_m[:, my_slot]], dsts=[T.land_m[:, my_slot] for c in to],
+                                              alu_op=0)], local_sem=S.snt)
+        sent += _bits(m_off)
+        g.wait_ge(S.ma, n_ma)
+        far = [partner[core]] + [partner[c] for c in nb]
+        g.remote_dma_fused([RemoteDMATransfer(dst_ids=[did(c) for c in far], dma_engine_mask=m_off, remote_sem=S.cmr,
+                                              srcs=all_slots, dsts=[T.cm_rem[:, :] for c in far], alu_op=2)],
+                           local_sem=S.snt)
+        sent += _bits(m_off)
+        g.remote_dma_fused([RemoteDMATransfer(dst_ids=[did(c) for c in nb], dma_engine_mask=m_rest, remote_sem=S.cmo,
+                                              srcs=all_slots, dsts=[T.cm_own[:, :] for c in nb], alu_op=2)],
+                           local_sem=S.snt)
+        sent += _bits(m_rest)
+        g.wait_ge(S.wn, _bits(topo.mask(nb[0], core)))
+        rid, pid = topo.addr(partner[nb[0]], core)
+        g.remote_dma(out_ap=T.wp_sb[:, :], in_ap=T.wn_sb[:, :], remote_sem=S.wp, local_sem=S.snt, pid=pid, routing_id=rid,
+                     dma_engine_mask=m_off)
+        sent += _bits(m_off)
+        V.wait_ge(S.ma, n_ma)
+        vop(V.tensor_tensor(T.G1[:, :], T.land_m[:, 0:16], T.land_m[:, 16:32], MAX))
+        vop(V.tensor_tensor(T.G2[:, :], T.G1[:, 0:8], T.G1[:, 8:16], MAX))
+        vop(V.tensor_tensor(T.cm_own[:, :], T.G2[:, 0:4], T.G2[:, 4:8], MAX))
+    else:
+        ow = owner_of[core]
+        rid, pid = topo.addr(ow, core)
+        g.remote_dma(out_ap=T.wn_sb[:, :], in_ap=T.w_sb[:, :], remote_sem=S.wn, local_sem=S.snt, pid=pid, routing_id=rid,
+                     dma_engine_mask=m_on)
+        sent += _bits(m_on)
+        g.wait_ge(S.v, n_piece)
+        g.remote_dma_fused([RemoteDMATransfer(dst_ids=[did(c) for c in owners], dma_engine_mask=m_on, remote_sem=S.ma,
+                                              srcs=[T.land_m[:, my_slot]], dsts=[T.land_m[:, my_slot] for c in owners],
+                                              alu_op=0)], local_sem=S.snt)
+        sent += _bits(m_on)
+        V.wait_ge(S.cmo, _bits(topo.mask(ow, core) & ~topo.mask(ow, partner[ow])))
+
+    V.wait_ge(S.cmr, n_far)
+    n_m = vop(V.tensor_tensor(T.m4[:, :], T.cm_own[:, :], T.cm_rem[:, :], MAX))
+    g.scalar.wait_ge(S.v, n_m)
+    g.scalar.dma_start(T.m[:, :], T.m4[:, :]).then_inc(S.stm, 16)
+    vop(V.tensor_copy(T.csp[:, 0:128:32], T.m4[:, :]))
+    vop(V.tensor_tensor(T.r1[:, :], T.m4[:, :], T.csp[:, 0:128:32], SUB))
+    vop(V.tensor_copy(T.csp[:, 1:128:32], T.r1[:, :]))
+    n_sp = vop(V.tensor_tensor(T.csp[:, 2:128:32], T.r1[:, :], T.csp[:, 1:128:32], SUB))
+    PE.wait_ge(S.idm, 32)
+    PE.wait_ge(S.v, n_sp)
+    PE.matmul(T.cTp[:, 0:128], T.csp[:, :], T.I_bf[:, :], True, True).then_inc(S.pT, 1)
+    V.wait_ge(S.pT, 1)
+    n_cT = vop(V.tensor_copy(T.cT[:, :], T.cTp[:, 0:128]))
+    PE.wait_ge(S.v, n_cT)
+
+    def minus_half_m(Z0, Z1, s0, s1):
+        for b in range(4):
+            Z, sm = (Z0, s0) if b < 2 else (Z1, s1)
+            c0 = 128 * (b % 2)
+            PE.matmul(Z[:, c0:c0 + 128], T.negh[:, 128 * b:128 * b + 128], T.cT[:, :], False, b % 2 == 1).then_inc(sm, 1)
+
+    def relu(R, Z0, Z1, s0, s1):
+        V.wait_ge(s0, 2)
+        n0 = vop(V.tensor_tensor(R[:, 0:256], Z0[:, 0:256], T.zero[:, :], MAX))
+        V.wait_ge(s1, 2)
+        n1 = vop(V.tensor_tensor(R[:, 256:512], Z1[:, 0:256], T.zero[:, :], MAX))
+        return n0, n1
+
+    def sums(out, R, n01, sm):
+        for b in range(4):
+            PE.wait_ge(S.v, n01[b // 2])
+            PE.matmul(out[:, b:b + 1], R[:, 128 * b:128 * b + 128], T.ones[:, 0:1], True, True).then_inc(sm, 1)
+
+    def keep_a():
+        V.wait_ge(S.psA, 4)
+        vop(V.tensor_copy(T.SA[:, :], T.Sp[:, 0:4]))
+
+    minus_half_m(T.ZA0, T.ZA1, S.pA0, S.pA1)
+    if early:
+        minus_half_m(T.ZB0, T.ZB1, S.pB0, S.pB1)
+        na = relu(T.RA, T.ZA0, T.ZA1, S.pA0, S.pA1)
+        nb_ = relu(T.RB, T.ZB0, T.ZB1, S.pB0, S.pB1)
+        sums(T.Sp, T.RA, na, S.psA)
+        sums(T.zT, T.RB, nb_, S.psB)
+        keep_a()
+    else:
+        na = relu(T.RA, T.ZA0, T.ZA1, S.pA0, S.pA1)
+        sums(T.Sp, T.RA, na, S.psA)
+        scores_b()
+        minus_half_m(T.ZB0, T.ZB1, S.pB0, S.pB1)
+        keep_a()
+        nb_ = relu(T.RB, T.ZB0, T.ZB1, S.pB0, S.pB1)
+        sums(T.zT, T.RB, nb_, S.psB)
+    V.wait_ge(S.psB, 4)
+    n_s = vop(V.tensor_tensor(T.land_s[:, my_slot], T.zT[:, 0:4], T.SA[:, :], ADD))
+
+    g.wait_ge(S.v, n_s)
+    g.remote_dma_fused([RemoteDMATransfer(dst_ids=[did(c) for c in peers], dma_engine_mask=m_on, remote_sem=S.sa,
+                                          srcs=[T.land_s[:, my_slot]], dsts=[T.land_s[:, my_slot] for c in peers],
+                                          alu_op=0)], local_sem=S.snt)
+    sent += _bits(m_on)
+    V.wait_ge(S.sa, sum(_bits(topo.mask(c, core)) for c in peers))
+    vop(V.tensor_tensor(T.A1[:, :], T.land_s[:, 0:16], T.land_s[:, 16:32], ADD))
+    vop(V.tensor_tensor(T.A2[:, :], T.A1[:, 0:8], T.A1[:, 8:16], ADD))
+    n_end = vop(V.tensor_tensor(T.s4[:, :], T.A2[:, 0:4], T.A2[:, 4:8], ADD))
+    g.sync.wait_ge(S.v, n_end)
+    g.sync.dma_start(T.s[:, :], T.s4[:, :]).then_inc(S.sts, 16)
+    g.wait_ge(S.snt, sent)
+    g.wait_ge(S.stm, 16)
+    g.wait_ge(S.sts, 16)

@@ -1,240 +1,192 @@
 from concourse.bass import DstId, RemoteDMATransfer
-from concourse.mybir import AluOpType
+from concourse.mybir import AluOpType, AxisListType, ActivationFunctionType
 
 F, B = "float32", "bfloat16"
+WORLD = 256
 SCRATCH = {
-    "h_sb": ("sbuf", [128, 512], B), "hp": ("sbuf", [128, 512], B),
-    "w_sb": ("sbuf", [128, 128], B), "wn_sb": ("sbuf", [128, 128], B), "wp_sb": ("sbuf", [128, 128], B),
-    "E": ("sbuf", [128, 129], B), "Dd": ("dram", [129, 128], B), "I_bf": ("sbuf", [128, 128], B),
-    "negh": ("sbuf", [128, 512], B), "csp": ("sbuf", [128, 128], B), "cT": ("sbuf", [128, 128], B),
-    "zero": ("sbuf", [128, 256], F), "ones": ("sbuf", [128, 4], F),
-    "zodd": ("sbuf", [128, 256], F), "S1": ("sbuf", [128, 128], F), "S2": ("sbuf", [128, 64], F),
-    "S3": ("sbuf", [128, 64], F), "S4": ("sbuf", [128, 32], F), "S5": ("sbuf", [128, 16], F), "S6": ("sbuf", [128, 8], F),
-    "land_m": ("sbuf", [128, 32], F), "G1": ("sbuf", [128, 16], F), "G2": ("sbuf", [128, 8], F),
-    "cm_own": ("sbuf", [128, 4], F), "cm_rem": ("sbuf", [128, 4], F), "m4": ("sbuf", [128, 4], F), "r1": ("sbuf", [128, 4], F),
-    "RA": ("sbuf", [128, 512], F), "RB": ("sbuf", [128, 512], F), "SA": ("sbuf", [128, 4], F),
+    "h_sb": ("sbuf", [128, 512], B), "w_sb": ("sbuf", [128, 128], B), "wn_sb": ("sbuf", [128, 128], B),
+    "wp_sb": ("sbuf", [128, 128], B),
+    "land_m": ("sbuf", [128, 32], F), "G1": ("sbuf", [128, 16], F), "G2": ("sbuf", [128, 8], F), "G3": ("sbuf", [128, 4], F),
+    "cm_rem": ("sbuf", [128, 4], F), "m4": ("sbuf", [128, 4], F), "nb": ("sbuf", [128, 4], F),
+    "RS": ("sbuf", [128, 768], F), "RV": ("sbuf", [128, 256], F), "acc": ("sbuf", [128, 8], F),
     "land_s": ("sbuf", [128, 32], F), "A1": ("sbuf", [128, 16], F), "A2": ("sbuf", [128, 8], F), "s4": ("sbuf", [128, 4], F),
-    "zT": ("psum", [128, 512], F), "P": ("psum", [128, 512], F), "cTp": ("psum", [128, 512], F), "Sp": ("psum", [128, 512], F),
-    "ZA0": ("psum", [128, 512], F), "ZA1": ("psum", [128, 512], F), "ZB0": ("psum", [128, 512], F), "ZB1": ("psum", [128, 512], F),
+    "ZA0": ("psum", [128, 512], F), "ZA1": ("psum", [128, 512], F), "ZA2": ("psum", [128, 512], F), "ZA3": ("psum", [128, 512], F),
+    "ZB0": ("psum", [128, 512], F), "ZB1": ("psum", [128, 512], F), "ZB2": ("psum", [128, 512], F), "ZB3": ("psum", [128, 512], F),
 }
-SEMAPHORES = ["lh", "lw", "idm", "v", "pz", "pT", "pA0", "pA1", "pB0", "pB1", "psA", "psB",
-              "wn", "wp", "ma", "cmo", "cmr", "sa", "snt", "stm", "sts"]
+SEMAPHORES = ["lh", "lw", "pa0", "pa1", "pa2", "pa3", "pb0", "pb1", "pb2", "pb3", "red", "g1", "g2", "g3", "mm", "nbs",
+              "act", "rv", "rr", "pc", "a1", "a2", "a3", "wn", "wp", "ma", "cmr", "sa", "snt", "stm", "sts"]
 
 
 def _bits(mask):
     return bin(mask).count("1")
 
 
+def _chips(T, topo):
+    cores = list(T.cores)
+    keys = sorted(set((topo.host(c), topo.chip(c)) for c in cores))
+    return [[c for c in cores if (topo.host(c), topo.chip(c)) == k] for k in keys]
+
+
 def _plan(topo, here, there):
+    group = list(here) + list(there)
     owners = [c for c in here if topo.may_write(c, there[0])]
-    owner_of, partner = {}, {}
+    owner_of, partner, helper = {}, {}, {}
     for d in sorted(set(topo.die(c) for c in here)):
         od = [c for c in owners if topo.die(c) == d]
         nd = [c for c in here if topo.die(c) == d and c not in owners]
-        for k, c in enumerate(nd):
-            owner_of[c] = od[k % len(od)]
         hd = [c for c in here if topo.die(c) == d]
         td = [c for c in there if topo.die(c) == d]
         for k, c in enumerate(hd):
             partner[c] = td[k]
-    return owners, owner_of, partner
+        for k, c in enumerate(nd):
+            owner_of[c] = od[k % len(od)]
+            idle = [x for x in range(WORLD) if x not in group and topo.die(x) == d and topo.same_plane(c, x)
+                    and topo.may_write(c, x) and topo.mates(x, partner[c]) and topo.may_write(x, partner[c])]
+            helper[c] = idle[k]
+    return owners, owner_of, partner, helper
 
 
 def rank_program(g, core, T, topo):
+    S, V, PE, ACT = T.sem, g.vector, g.tensor, g.scalar
+    MAX, ADD, MUL = AluOpType.max, AluOpType.add, AluOpType.mult
+    X = AxisListType.X
+    chip_a, chip_b = _chips(T, topo)
+
     if T.rank_of(core) is None:
+        for here, there in ((chip_a, chip_b), (chip_b, chip_a)):
+            _, _, partner, helper = _plan(topo, here, there)
+            for c in here:
+                if helper.get(c) == core:
+                    mk = topo.mask(core, partner[c])
+                    rid, pid = topo.addr(partner[c], core)
+                    g.wait_ge(S.wn, _bits(topo.mask(c, core)))
+                    g.remote_dma(out_ap=T.wp_sb[:, :], in_ap=T.wn_sb[:, :], remote_sem=S.wp, local_sem=S.snt, pid=pid,
+                                 routing_id=rid, dma_engine_mask=mk)
+                    g.wait_ge(S.snt, _bits(mk))
         return
-    S, V, PE = T.sem, g.vector, g.tensor
-    MAX, ADD, SUB = AluOpType.max, AluOpType.add, AluOpType.subtract
-    cores = list(T.cores)
-    mine = [c for c in cores if (topo.host(c), topo.chip(c)) == (topo.host(core), topo.chip(core))]
-    other = [c for c in cores if c not in mine]
-    owners, owner_of, partner = _plan(topo, mine, other)
-    owners_o, owner_of_o, partner_o = _plan(topo, other, mine)
+
+    mine, other = (chip_a, chip_b) if core in chip_a else (chip_b, chip_a)
+    owners, owner_of, partner, helper = _plan(topo, mine, other)
+    owners_o, owner_of_o, partner_o, helper_o = _plan(topo, other, mine)
     is_owner = core in owners
     slot = mine.index(core)
     my_slot = slice(4 * slot, 4 * slot + 4)
-    wsrc = [c for c in other if partner_o[c] == core][0]
-    early = wsrc in owners_o
-    wfrom = wsrc if early else owner_of_o[wsrc]
-    n_far = _bits(topo.mask(wfrom, core))
     peers = [c for c in mine if c != core]
     m_on = topo.mask(core, peers[0])
+    wsrc = [c for c in other if partner_o[c] == core][0]
+    n_wp = _bits(topo.mask(wsrc if wsrc in owners_o else helper_o[wsrc], core))
+    n_cmr = _bits(topo.mask(wsrc if wsrc in owners_o else owner_of_o[wsrc], core))
+    ZA = [T["ZA%d" % b] for b in range(4)]
+    ZB = [T["ZB%d" % b] for b in range(4)]
 
     def did(d):
         rid, pid = topo.addr(d, core)
         return DstId(rid=rid, pnc=pid)
 
-    nv = [0]
+    def piece_mask(c, d):
+        on = topo.mask(c, d)
+        if c not in owners:
+            return on
+        off = topo.mask(c, partner[c])
+        return (on & off) if d in owners else (on & ~off)
 
-    def vop(ins):
-        ins.then_inc(S.v, 1)
-        nv[0] += 1
-        V.wait_ge(S.v, nv[0])
-        return nv[0]
+    def copy_to(dsts, buf, mask, sem):
+        return RemoteDMATransfer(dst_ids=[did(c) for c in dsts], dma_engine_mask=mask, remote_sem=sem,
+                                 srcs=[buf[:, my_slot]], dsts=[buf[:, my_slot] for c in dsts], alu_op=0)
+
+    n_ma = sum(_bits(piece_mask(c, core)) for c in peers)
 
     g.sync.dma_start(T.h_sb[:, :], T.h[:, :]).then_inc(S.lh, 16)
-    g.scalar.dma_start(T.w_sb[:, :], T.w[:, :]).then_inc(S.lw, 16)
-
-    vop(V.memset(T.E[:, :], 0.0))
-    n_E = vop(V.memset(T.E[:, 0:1], 1.0))
-    vop(V.memset(T.csp[:, :], 0.0))
-    vop(V.memset(T.negh[:, :], 0.0))
-    for b in range(4):
-        vop(V.memset(T.negh[32 * b:32 * b + 32, 128 * b:128 * b + 128], -0.5))
-    vop(V.memset(T.ones[:, :], 1.0))
-    vop(V.memset(T.zero[:, :], 0.0))
-    g.sync.wait_ge(S.v, n_E)
-    g.sync.dma_start(T.Dd[:, :], T.E[:, :]).then_inc(S.idm, 16)
-    g.sync.wait_ge(S.idm, 16)
-    g.sync.dma_start(T.I_bf[:, :], T.Dd[0:128, :]).then_inc(S.idm, 16)
+    ACT.dma_start(T.w_sb[:, :], T.w[:, :]).then_inc(S.lw, 16)
 
     PE.wait_ge(S.lh, 16)
     PE.wait_ge(S.lw, 16)
     for b in range(4):
-        PE.matmul(T.zT[:, 128 * b:128 * b + 128], T.h_sb[:, b:512:4], T.w_sb[:, :], True, True).then_inc(S.pz, 1)
-    V.wait_ge(S.pz, 4)
-    vop(V.tensor_copy(T.zodd[:, :], T.zT[:, 1:512:2]))
-    vop(V.tensor_tensor(T.P[:, 0:128], T.zT[:, 0:512:4], T.zodd[:, 0:256:2], MAX))
-    vop(V.tensor_tensor(T.S1[:, :], T.zT[:, 2:512:4], T.zodd[:, 1:256:2], MAX))
-    vop(V.tensor_tensor(T.P[:, 128:192], T.P[:, 0:128:2], T.S1[:, 0:128:2], MAX))
-    vop(V.tensor_tensor(T.S2[:, :], T.P[:, 1:128:2], T.S1[:, 1:128:2], MAX))
-    vop(V.tensor_tensor(T.S3[:, :], T.P[:, 128:192], T.S2[:, :], MAX))
-    vop(V.tensor_tensor(T.S4[:, :], T.S3[:, 0:64:2], T.S3[:, 1:64:2], MAX))
-    vop(V.tensor_tensor(T.S5[:, :], T.S4[:, 0:32:2], T.S4[:, 1:32:2], MAX))
-    vop(V.tensor_tensor(T.S6[:, :], T.S5[:, 0:16:2], T.S5[:, 1:16:2], MAX))
-    n_piece = vop(V.tensor_tensor(T.land_m[:, my_slot], T.S6[:, 0:8:2], T.S6[:, 1:8:2], MAX))
+        PE.matmul(ZA[b][:, 0:128], T.h_sb[:, b:512:4], T.w_sb[:, :], True, True).then_inc(S["pa%d" % b], 1)
+    PE.wait_ge(S.wp, n_wp)
+    for b in range(4):
+        PE.matmul(ZB[b][:, 0:128], T.h_sb[:, b:512:4], T.wp_sb[:, :], True, True).then_inc(S["pb%d" % b], 1)
 
     for b in range(4):
-        n_hp = vop(V.tensor_copy(T.hp[:, 128 * b:128 * b + 128], T.h_sb[:, b:512:4]))
-    PE.wait_ge(S.v, n_hp)
-    PE.matmul(T.ZA0[:, 0:256], T.w_sb[:, :], T.hp[:, 0:256], True, False)
-    PE.matmul(T.ZA1[:, 0:256], T.w_sb[:, :], T.hp[:, 256:512], True, False)
-
-    def scores_b():
-        PE.wait_ge(S.wp, n_far)
-        PE.matmul(T.ZB0[:, 0:256], T.wp_sb[:, :], T.hp[:, 0:256], True, False)
-        PE.matmul(T.ZB1[:, 0:256], T.wp_sb[:, :], T.hp[:, 256:512], True, False)
-
-    if early:
-        scores_b()
+        V.wait_ge(S["pa%d" % b], 1)
+        V.tensor_reduce(T.land_m[:, 4 * slot + b:4 * slot + b + 1], ZA[b][:, 0:128], X, MAX).then_inc(S.red, 1)
 
     sent = 0
-    all_slots = [T.land_m[:, 4 * k:4 * k + 4] for k in range(len(mine))]
     g.wait_ge(S.lw, 16)
     if is_owner:
-        nb = [c for c in mine if owner_of.get(c) == core]
         m_off = topo.mask(core, partner[core])
-        m_rest = m_on & ~m_off
-        n_ma = sum(_bits(topo.mask(c, core) & (topo.mask(c, partner[c]) if c in owners else topo.mask(c, core)))
-                   for c in peers)
         rid, pid = topo.addr(partner[core], core)
         g.remote_dma(out_ap=T.wp_sb[:, :], in_ap=T.w_sb[:, :], remote_sem=S.wp, local_sem=S.snt, pid=pid, routing_id=rid,
                      dma_engine_mask=m_off)
         sent += _bits(m_off)
-        g.wait_ge(S.v, n_piece)
-        to = [c for c in owners if c != core]
-        g.remote_dma_fused([RemoteDMATransfer(dst_ids=[did(c) for c in to], dma_engine_mask=m_off, remote_sem=S.ma,
-                                              srcs=[T.land_m[:, my_slot]], dsts=[T.land_m[:, my_slot] for c in to],
-                                              alu_op=0)], local_sem=S.snt)
-        sent += _bits(m_off)
+        g.wait_ge(S.red, 4)
+        to_o = [c for c in owners if c != core]
+        to_n = [c for c in peers if c not in owners]
+        g.remote_dma_fused([copy_to(to_o, T.land_m, piece_mask(core, to_o[0]), S.ma),
+                            copy_to(to_n, T.land_m, piece_mask(core, to_n[0]), S.ma)], local_sem=S.snt)
+        sent += _bits(piece_mask(core, to_o[0])) + _bits(piece_mask(core, to_n[0]))
         g.wait_ge(S.ma, n_ma)
-        far = [partner[core]] + [partner[c] for c in nb]
+        far = [partner[core]] + [partner[c] for c in mine if owner_of.get(c) == core]
         g.remote_dma_fused([RemoteDMATransfer(dst_ids=[did(c) for c in far], dma_engine_mask=m_off, remote_sem=S.cmr,
-                                              srcs=all_slots, dsts=[T.cm_rem[:, :] for c in far], alu_op=2)],
-                           local_sem=S.snt)
+                                              srcs=[T.land_m[:, 4 * k:4 * k + 4] for k in range(len(mine))],
+                                              dsts=[T.cm_rem[:, :] for c in far], alu_op=2)], local_sem=S.snt)
         sent += _bits(m_off)
-        g.remote_dma_fused([RemoteDMATransfer(dst_ids=[did(c) for c in nb], dma_engine_mask=m_rest, remote_sem=S.cmo,
-                                              srcs=all_slots, dsts=[T.cm_own[:, :] for c in nb], alu_op=2)],
-                           local_sem=S.snt)
-        sent += _bits(m_rest)
-        g.wait_ge(S.wn, _bits(topo.mask(nb[0], core)))
-        rid, pid = topo.addr(partner[nb[0]], core)
-        g.remote_dma(out_ap=T.wp_sb[:, :], in_ap=T.wn_sb[:, :], remote_sem=S.wp, local_sem=S.snt, pid=pid, routing_id=rid,
-                     dma_engine_mask=m_off)
-        sent += _bits(m_off)
-        V.wait_ge(S.ma, n_ma)
-        vop(V.tensor_tensor(T.G1[:, :], T.land_m[:, 0:16], T.land_m[:, 16:32], MAX))
-        vop(V.tensor_tensor(T.G2[:, :], T.G1[:, 0:8], T.G1[:, 8:16], MAX))
-        vop(V.tensor_tensor(T.cm_own[:, :], T.G2[:, 0:4], T.G2[:, 4:8], MAX))
     else:
-        ow = owner_of[core]
-        rid, pid = topo.addr(ow, core)
+        hp = helper[core]
+        m_hp = topo.mask(core, hp)
+        rid, pid = topo.addr(hp, core)
         g.remote_dma(out_ap=T.wn_sb[:, :], in_ap=T.w_sb[:, :], remote_sem=S.wn, local_sem=S.snt, pid=pid, routing_id=rid,
-                     dma_engine_mask=m_on)
-        sent += _bits(m_on)
-        g.wait_ge(S.v, n_piece)
-        g.remote_dma_fused([RemoteDMATransfer(dst_ids=[did(c) for c in owners], dma_engine_mask=m_on, remote_sem=S.ma,
-                                              srcs=[T.land_m[:, my_slot]], dsts=[T.land_m[:, my_slot] for c in owners],
-                                              alu_op=0)], local_sem=S.snt)
-        sent += _bits(m_on)
-        V.wait_ge(S.cmo, _bits(topo.mask(ow, core) & ~topo.mask(ow, partner[ow])))
+                     dma_engine_mask=m_hp)
+        sent += _bits(m_hp)
+        g.wait_ge(S.red, 4)
+        g.remote_dma_fused([copy_to(owners, T.land_m, m_on, S.ma)], local_sem=S.snt)
+        g.remote_dma_fused([copy_to([c for c in peers if c not in owners], T.land_m, m_on, S.ma)], local_sem=S.snt)
+        sent += 2 * _bits(m_on)
 
-    V.wait_ge(S.cmr, n_far)
-    n_m = vop(V.tensor_tensor(T.m4[:, :], T.cm_own[:, :], T.cm_rem[:, :], MAX))
-    g.scalar.wait_ge(S.v, n_m)
-    g.scalar.dma_start(T.m[:, :], T.m4[:, :]).then_inc(S.stm, 16)
-    vop(V.tensor_copy(T.csp[:, 0:128:32], T.m4[:, :]))
-    vop(V.tensor_tensor(T.r1[:, :], T.m4[:, :], T.csp[:, 0:128:32], SUB))
-    vop(V.tensor_copy(T.csp[:, 1:128:32], T.r1[:, :]))
-    n_sp = vop(V.tensor_tensor(T.csp[:, 2:128:32], T.r1[:, :], T.csp[:, 1:128:32], SUB))
-    PE.wait_ge(S.idm, 32)
-    PE.wait_ge(S.v, n_sp)
-    PE.matmul(T.cTp[:, 0:128], T.csp[:, :], T.I_bf[:, :], True, True).then_inc(S.pT, 1)
-    V.wait_ge(S.pT, 1)
-    n_cT = vop(V.tensor_copy(T.cT[:, :], T.cTp[:, 0:128]))
-    PE.wait_ge(S.v, n_cT)
+    V.wait_ge(S.red, 4)
+    V.wait_ge(S.ma, n_ma)
+    V.tensor_tensor(T.G1[:, :], T.land_m[:, 0:16], T.land_m[:, 16:32], MAX).then_inc(S.g1, 1)
+    V.wait_ge(S.g1, 1)
+    V.tensor_tensor(T.G2[:, :], T.G1[:, 0:8], T.G1[:, 8:16], MAX).then_inc(S.g2, 1)
+    V.wait_ge(S.g2, 1)
+    V.tensor_tensor(T.G3[:, :], T.G2[:, 0:4], T.G2[:, 4:8], MAX).then_inc(S.g3, 1)
+    V.wait_ge(S.g3, 1)
+    V.wait_ge(S.cmr, n_cmr)
+    V.tensor_tensor(T.m4[:, :], T.G3[:, :], T.cm_rem[:, :], MAX).then_inc(S.mm, 1)
+    V.wait_ge(S.mm, 1)
+    V.tensor_scalar(T.nb[:, :], T.m4[:, :], -0.5, None, MUL).then_inc(S.nbs, 1)
+    g.sync.wait_ge(S.mm, 1)
+    g.sync.dma_start(T.m[:, :], T.m4[:, :]).then_inc(S.stm, 16)
 
-    def minus_half_m(Z0, Z1, s0, s1):
-        for b in range(4):
-            Z, sm = (Z0, s0) if b < 2 else (Z1, s1)
-            c0 = 128 * (b % 2)
-            PE.matmul(Z[:, c0:c0 + 128], T.negh[:, 128 * b:128 * b + 128], T.cT[:, :], False, b % 2 == 1).then_inc(sm, 1)
+    ACT.wait_ge(S.nbs, 1)
+    for k in range(6):
+        b = k % 4
+        if k >= 4:
+            ACT.wait_ge(S["pb%d" % b], 1)
+        ACT.activation(T.RS[:, 128 * k:128 * k + 128], (ZA if k < 4 else ZB)[b][:, 0:128], ActivationFunctionType.Relu,
+                       bias=T.nb[:, b:b + 1], scale=1.0, accum_out=T.acc[:, k:k + 1]).then_inc(S.act, 1)
+    V.wait_ge(S.nbs, 1)
+    for b in (2, 3):
+        V.wait_ge(S["pb%d" % b], 1)
+        V.tensor_scalar(T.RV[:, 128 * (b - 2):128 * (b - 1)], ZB[b][:, 0:128], T.nb[:, b:b + 1], 0.0, ADD, MAX).then_inc(S.rv, 1)
+    V.wait_ge(S.rv, 2)
+    for b in (2, 3):
+        V.tensor_reduce(T.acc[:, 4 + b:5 + b], T.RV[:, 128 * (b - 2):128 * (b - 1)], X, ADD).then_inc(S.rr, 1)
+    V.wait_ge(S.rr, 2)
+    V.wait_ge(S.act, 6)
+    V.tensor_tensor(T.land_s[:, my_slot], T.acc[:, 0:4], T.acc[:, 4:8], ADD).then_inc(S.pc, 1)
 
-    def relu(R, Z0, Z1, s0, s1):
-        V.wait_ge(s0, 2)
-        n0 = vop(V.tensor_tensor(R[:, 0:256], Z0[:, 0:256], T.zero[:, :], MAX))
-        V.wait_ge(s1, 2)
-        n1 = vop(V.tensor_tensor(R[:, 256:512], Z1[:, 0:256], T.zero[:, :], MAX))
-        return n0, n1
-
-    def sums(out, R, n01, sm):
-        for b in range(4):
-            PE.wait_ge(S.v, n01[b // 2])
-            PE.matmul(out[:, b:b + 1], R[:, 128 * b:128 * b + 128], T.ones[:, 0:1], True, True).then_inc(sm, 1)
-
-    def keep_a():
-        V.wait_ge(S.psA, 4)
-        vop(V.tensor_copy(T.SA[:, :], T.Sp[:, 0:4]))
-
-    minus_half_m(T.ZA0, T.ZA1, S.pA0, S.pA1)
-    if early:
-        minus_half_m(T.ZB0, T.ZB1, S.pB0, S.pB1)
-        na = relu(T.RA, T.ZA0, T.ZA1, S.pA0, S.pA1)
-        nb_ = relu(T.RB, T.ZB0, T.ZB1, S.pB0, S.pB1)
-        sums(T.Sp, T.RA, na, S.psA)
-        sums(T.zT, T.RB, nb_, S.psB)
-        keep_a()
-    else:
-        na = relu(T.RA, T.ZA0, T.ZA1, S.pA0, S.pA1)
-        sums(T.Sp, T.RA, na, S.psA)
-        scores_b()
-        minus_half_m(T.ZB0, T.ZB1, S.pB0, S.pB1)
-        keep_a()
-        nb_ = relu(T.RB, T.ZB0, T.ZB1, S.pB0, S.pB1)
-        sums(T.zT, T.RB, nb_, S.psB)
-    V.wait_ge(S.psB, 4)
-    n_s = vop(V.tensor_tensor(T.land_s[:, my_slot], T.zT[:, 0:4], T.SA[:, :], ADD))
-
-    g.wait_ge(S.v, n_s)
-    g.remote_dma_fused([RemoteDMATransfer(dst_ids=[did(c) for c in peers], dma_engine_mask=m_on, remote_sem=S.sa,
-                                          srcs=[T.land_s[:, my_slot]], dsts=[T.land_s[:, my_slot] for c in peers],
-                                          alu_op=0)], local_sem=S.snt)
+    g.wait_ge(S.pc, 1)
+    g.remote_dma_fused([copy_to(peers, T.land_s, m_on, S.sa)], local_sem=S.snt)
     sent += _bits(m_on)
+    V.wait_ge(S.pc, 1)
     V.wait_ge(S.sa, sum(_bits(topo.mask(c, core)) for c in peers))
-    vop(V.tensor_tensor(T.A1[:, :], T.land_s[:, 0:16], T.land_s[:, 16:32], ADD))
-    vop(V.tensor_tensor(T.A2[:, :], T.A1[:, 0:8], T.A1[:, 8:16], ADD))
-    n_end = vop(V.tensor_tensor(T.s4[:, :], T.A2[:, 0:4], T.A2[:, 4:8], ADD))
-    g.sync.wait_ge(S.v, n_end)
+    V.tensor_tensor(T.A1[:, :], T.land_s[:, 0:16], T.land_s[:, 16:32], ADD).then_inc(S.a1, 1)
+    V.wait_ge(S.a1, 1)
+    V.tensor_tensor(T.A2[:, :], T.A1[:, 0:8], T.A1[:, 8:16], ADD).then_inc(S.a2, 1)
+    V.wait_ge(S.a2, 1)
+    V.tensor_tensor(T.s4[:, :], T.A2[:, 0:4], T.A2[:, 4:8], ADD).then_inc(S.a3, 1)
+    g.sync.wait_ge(S.a3, 1)
     g.sync.dma_start(T.s[:, :], T.s4[:, :]).then_inc(S.sts, 16)
     g.wait_ge(S.snt, sent)
     g.wait_ge(S.stm, 16)

@@ -7,14 +7,15 @@ SCRATCH = {
     "h_sb": ("sbuf", [128, 512], B), "w_sb": ("sbuf", [128, 128], B), "wn_sb": ("sbuf", [128, 128], B),
     "wp_sb": ("sbuf", [128, 128], B),
     "land_m": ("sbuf", [128, 32], F), "G1": ("sbuf", [128, 16], F), "G2": ("sbuf", [128, 8], F), "G3": ("sbuf", [128, 4], F),
+    "G3h": ("sbuf", [128, 4], F),
     "cm_rem": ("sbuf", [128, 4], F), "m4": ("sbuf", [128, 4], F), "nb": ("sbuf", [128, 4], F),
-    "RS": ("sbuf", [128, 768], F), "RV": ("sbuf", [128, 256], F), "acc": ("sbuf", [128, 8], F),
-    "land_s": ("sbuf", [128, 32], F), "A1": ("sbuf", [128, 16], F), "A2": ("sbuf", [128, 8], F), "s4": ("sbuf", [128, 4], F),
+    "RS": ("sbuf", [128, 768], F), "RV": ("sbuf", [128, 256], F),
+    "land_s": ("sbuf", [128, 64], F), "J": ("sbuf", [128, 32], F), "s4": ("sbuf", [128, 4], F),
     "ZA0": ("psum", [128, 512], F), "ZA1": ("psum", [128, 512], F), "ZA2": ("psum", [128, 512], F), "ZA3": ("psum", [128, 512], F),
     "ZB0": ("psum", [128, 512], F), "ZB1": ("psum", [128, 512], F), "ZB2": ("psum", [128, 512], F), "ZB3": ("psum", [128, 512], F),
 }
-SEMAPHORES = ["lh", "lw", "pa0", "pa1", "pa2", "pa3", "pb0", "pb1", "pb2", "pb3", "red", "g1", "g2", "g3", "mm", "nbs",
-              "act", "rv", "rr", "pc", "a1", "a2", "a3", "wn", "wp", "ma", "cmr", "sa", "snt", "stm", "sts"]
+SEMAPHORES = ["lh", "lw", "pa0", "pa1", "pa2", "pa3", "pb0", "pb1", "pb2", "pb3", "red", "g1", "g2", "g3", "g3h", "mm",
+              "nb0", "nb1", "nb2", "nb3", "act", "rv", "rr", "fv", "fa", "wn", "wp", "ma", "cmr", "sa", "snt", "stm", "sts"]
 
 
 def _bits(mask):
@@ -48,7 +49,7 @@ def _plan(topo, here, there):
 
 def rank_program(g, core, T, topo):
     S, V, PE, ACT = T.sem, g.vector, g.tensor, g.scalar
-    MAX, ADD, MUL = AluOpType.max, AluOpType.add, AluOpType.mult
+    MAX, MIN, ADD, MUL = AluOpType.max, AluOpType.min, AluOpType.add, AluOpType.mult
     X = AxisListType.X
     chip_a, chip_b = _chips(T, topo)
 
@@ -70,7 +71,8 @@ def rank_program(g, core, T, topo):
     owners_o, owner_of_o, partner_o, helper_o = _plan(topo, other, mine)
     is_owner = core in owners
     slot = mine.index(core)
-    my_slot = slice(4 * slot, 4 * slot + 4)
+    m_slot = slice(4 * slot, 4 * slot + 4)
+    s_slot = slice(8 * slot, 8 * slot + 8)
     peers = [c for c in mine if c != core]
     m_on = topo.mask(core, peers[0])
     wsrc = [c for c in other if partner_o[c] == core][0]
@@ -90,9 +92,9 @@ def rank_program(g, core, T, topo):
         off = topo.mask(c, partner[c])
         return (on & off) if d in owners else (on & ~off)
 
-    def copy_to(dsts, buf, mask, sem):
+    def copy_to(dsts, buf, cols, mask, sem):
         return RemoteDMATransfer(dst_ids=[did(c) for c in dsts], dma_engine_mask=mask, remote_sem=sem,
-                                 srcs=[buf[:, my_slot]], dsts=[buf[:, my_slot] for c in dsts], alu_op=0)
+                                 srcs=[buf[:, cols]], dsts=[buf[:, cols] for c in dsts], alu_op=0)
 
     n_ma = sum(_bits(piece_mask(c, core)) for c in peers)
 
@@ -104,7 +106,7 @@ def rank_program(g, core, T, topo):
     for b in range(4):
         PE.matmul(ZA[b][:, 0:128], T.h_sb[:, b:512:4], T.w_sb[:, :], True, True).then_inc(S["pa%d" % b], 1)
     PE.wait_ge(S.wp, n_wp)
-    for b in range(4):
+    for b in (2, 3, 0, 1):
         PE.matmul(ZB[b][:, 0:128], T.h_sb[:, b:512:4], T.wp_sb[:, :], True, True).then_inc(S["pb%d" % b], 1)
 
     for b in range(4):
@@ -122,8 +124,8 @@ def rank_program(g, core, T, topo):
         g.wait_ge(S.red, 4)
         to_o = [c for c in owners if c != core]
         to_n = [c for c in peers if c not in owners]
-        g.remote_dma_fused([copy_to(to_o, T.land_m, piece_mask(core, to_o[0]), S.ma),
-                            copy_to(to_n, T.land_m, piece_mask(core, to_n[0]), S.ma)], local_sem=S.snt)
+        g.remote_dma_fused([copy_to(to_o, T.land_m, m_slot, piece_mask(core, to_o[0]), S.ma),
+                            copy_to(to_n, T.land_m, m_slot, piece_mask(core, to_n[0]), S.ma)], local_sem=S.snt)
         sent += _bits(piece_mask(core, to_o[0])) + _bits(piece_mask(core, to_n[0]))
         g.wait_ge(S.ma, n_ma)
         far = [partner[core]] + [partner[c] for c in mine if owner_of.get(c) == core]
@@ -139,8 +141,8 @@ def rank_program(g, core, T, topo):
                      dma_engine_mask=m_hp)
         sent += _bits(m_hp)
         g.wait_ge(S.red, 4)
-        g.remote_dma_fused([copy_to(owners, T.land_m, m_on, S.ma)], local_sem=S.snt)
-        g.remote_dma_fused([copy_to([c for c in peers if c not in owners], T.land_m, m_on, S.ma)], local_sem=S.snt)
+        g.remote_dma_fused([copy_to(owners, T.land_m, m_slot, m_on, S.ma)], local_sem=S.snt)
+        g.remote_dma_fused([copy_to([c for c in peers if c not in owners], T.land_m, m_slot, m_on, S.ma)], local_sem=S.snt)
         sent += 2 * _bits(m_on)
 
     V.wait_ge(S.red, 4)
@@ -151,42 +153,49 @@ def rank_program(g, core, T, topo):
     V.wait_ge(S.g2, 1)
     V.tensor_tensor(T.G3[:, :], T.G2[:, 0:4], T.G2[:, 4:8], MAX).then_inc(S.g3, 1)
     V.wait_ge(S.g3, 1)
+    V.tensor_scalar(T.G3h[:, :], T.G3[:, :], -0.5, None, MUL).then_inc(S.g3h, 1)
+    V.wait_ge(S.g3h, 1)
     V.wait_ge(S.cmr, n_cmr)
+    for b in range(4):
+        V.tensor_scalar(T.nb[:, b:b + 1], T.cm_rem[:, b:b + 1], -0.5, T.G3h[:, b:b + 1], MUL, MIN).then_inc(S["nb%d" % b], 1)
     V.tensor_tensor(T.m4[:, :], T.G3[:, :], T.cm_rem[:, :], MAX).then_inc(S.mm, 1)
-    V.wait_ge(S.mm, 1)
-    V.tensor_scalar(T.nb[:, :], T.m4[:, :], -0.5, None, MUL).then_inc(S.nbs, 1)
     g.sync.wait_ge(S.mm, 1)
     g.sync.dma_start(T.m[:, :], T.m4[:, :]).then_inc(S.stm, 16)
 
-    ACT.wait_ge(S.nbs, 1)
     for k in range(6):
         b = k % 4
-        if k >= 4:
-            ACT.wait_ge(S["pb%d" % b], 1)
+        ACT.wait_ge(S["nb%d" % b] if k < 4 else S["pb%d" % b], 1)
         ACT.activation(T.RS[:, 128 * k:128 * k + 128], (ZA if k < 4 else ZB)[b][:, 0:128], ActivationFunctionType.Relu,
-                       bias=T.nb[:, b:b + 1], scale=1.0, accum_out=T.acc[:, k:k + 1]).then_inc(S.act, 1)
-    V.wait_ge(S.nbs, 1)
+                       bias=T.nb[:, b:b + 1], scale=1.0,
+                       accum_out=T.land_s[:, 8 * slot + k:8 * slot + k + 1]).then_inc(S.act, 1)
     for b in (2, 3):
+        V.wait_ge(S["nb%d" % b], 1)
         V.wait_ge(S["pb%d" % b], 1)
         V.tensor_scalar(T.RV[:, 128 * (b - 2):128 * (b - 1)], ZB[b][:, 0:128], T.nb[:, b:b + 1], 0.0, ADD, MAX).then_inc(S.rv, 1)
     V.wait_ge(S.rv, 2)
     for b in (2, 3):
-        V.tensor_reduce(T.acc[:, 4 + b:5 + b], T.RV[:, 128 * (b - 2):128 * (b - 1)], X, ADD).then_inc(S.rr, 1)
+        V.tensor_reduce(T.land_s[:, 8 * slot + 4 + b:8 * slot + 5 + b], T.RV[:, 128 * (b - 2):128 * (b - 1)], X,
+                        ADD).then_inc(S.rr, 1)
+
+    g.wait_ge(S.act, 6)
+    g.wait_ge(S.rr, 2)
+    g.remote_dma_fused([copy_to(peers, T.land_s, s_slot, m_on, S.sa)], local_sem=S.snt)
+    sent += _bits(m_on)
+
+    n_sa = sum(_bits(topo.mask(c, core)) for c in peers)
     V.wait_ge(S.rr, 2)
     V.wait_ge(S.act, 6)
-    V.tensor_tensor(T.land_s[:, my_slot], T.acc[:, 0:4], T.acc[:, 4:8], ADD).then_inc(S.pc, 1)
-
-    g.wait_ge(S.pc, 1)
-    g.remote_dma_fused([copy_to(peers, T.land_s, m_on, S.sa)], local_sem=S.snt)
-    sent += _bits(m_on)
-    V.wait_ge(S.pc, 1)
-    V.wait_ge(S.sa, sum(_bits(topo.mask(c, core)) for c in peers))
-    V.tensor_tensor(T.A1[:, :], T.land_s[:, 0:16], T.land_s[:, 16:32], ADD).then_inc(S.a1, 1)
-    V.wait_ge(S.a1, 1)
-    V.tensor_tensor(T.A2[:, :], T.A1[:, 0:8], T.A1[:, 8:16], ADD).then_inc(S.a2, 1)
-    V.wait_ge(S.a2, 1)
-    V.tensor_tensor(T.s4[:, :], T.A2[:, 0:4], T.A2[:, 4:8], ADD).then_inc(S.a3, 1)
-    g.sync.wait_ge(S.a3, 1)
+    V.wait_ge(S.sa, n_sa)
+    for b in (0, 1):
+        V.tensor_reduce(T.s4[:, b:b + 1], T.land_s[:, b:64:4], X, ADD).then_inc(S.fv, 1)
+    ACT.wait_ge(S.act, 6)
+    ACT.wait_ge(S.rr, 2)
+    ACT.wait_ge(S.sa, n_sa)
+    for b in (2, 3):
+        ACT.activation(T.J[:, 16 * (b - 2):16 * (b - 1)], T.land_s[:, b:64:4], ActivationFunctionType.Identity,
+                       accum_out=T.s4[:, b:b + 1]).then_inc(S.fa, 1)
+    g.sync.wait_ge(S.fv, 2)
+    g.sync.wait_ge(S.fa, 2)
     g.sync.dma_start(T.s[:, :], T.s4[:, :]).then_inc(S.sts, 16)
     g.wait_ge(S.snt, sent)
     g.wait_ge(S.stm, 16)

from concourse.bass import DstId, RemoteDMATransfer
from concourse.mybir import AluOpType, AxisListType, ActivationFunctionType

F, B = "float32", "bfloat16"
WORLD = 256
SCRATCH = {
    "h_sb": ("sbuf", [128, 512], B), "w_sb": ("sbuf", [128, 128], B), "wn_sb": ("sbuf", [128, 128], B),
    "wp_sb": ("sbuf", [128, 128], B),
    "land_m": ("sbuf", [128, 32], F), "G1": ("sbuf", [128, 16], F), "G2": ("sbuf", [128, 8], F), "G3": ("sbuf", [128, 4], F),
    "G3h": ("sbuf", [128, 4], F),
    "cm_rem": ("sbuf", [128, 4], F), "m4": ("sbuf", [128, 4], F), "nb": ("sbuf", [128, 4], F),
    "RS": ("sbuf", [128, 768], F), "RV": ("sbuf", [128, 256], F),
    "land_s": ("sbuf", [128, 64], F), "J": ("sbuf", [128, 32], F), "s4": ("sbuf", [128, 4], F),
    "ZA0": ("psum", [128, 512], F), "ZA1": ("psum", [128, 512], F), "ZA2": ("psum", [128, 512], F), "ZA3": ("psum", [128, 512], F),
    "ZB0": ("psum", [128, 512], F), "ZB1": ("psum", [128, 512], F), "ZB2": ("psum", [128, 512], F), "ZB3": ("psum", [128, 512], F),
}
SEMAPHORES = ["lh", "lw", "pa0", "pa1", "pa2", "pa3", "pb0", "pb1", "pb2", "pb3", "red", "g1", "g2", "g3", "g3h", "mm",
              "nb0", "nb1", "nb2", "nb3", "act", "rv", "rr", "fv", "fa", "wn", "wp", "ma", "cmr", "sa", "snt", "stm", "sts"]


def _bits(mask):
    return bin(mask).count("1")


def _chips(T, topo):
    cores = list(T.cores)
    keys = sorted(set((topo.host(c), topo.chip(c)) for c in cores))
    return [[c for c in cores if (topo.host(c), topo.chip(c)) == k] for k in keys]


def _plan(topo, here, there):
    group = list(here) + list(there)
    owners = [c for c in here if topo.may_write(c, there[0])]
    owner_of, partner, helper = {}, {}, {}
    for d in sorted(set(topo.die(c) for c in here)):
        od = [c for c in owners if topo.die(c) == d]
        nd = [c for c in here if topo.die(c) == d and c not in owners]
        hd = [c for c in here if topo.die(c) == d]
        td = [c for c in there if topo.die(c) == d]
        for k, c in enumerate(hd):
            partner[c] = td[k]
        for k, c in enumerate(nd):
            owner_of[c] = od[k % len(od)]
            idle = [x for x in range(WORLD) if x not in group and topo.die(x) == d and topo.same_plane(c, x)
                    and topo.may_write(c, x) and topo.mates(x, partner[c]) and topo.may_write(x, partner[c])]
            helper[c] = idle[k]
    return owners, owner_of, partner, helper


def rank_program(g, core, T, topo):
    S, V, PE, ACT = T.sem, g.vector, g.tensor, g.scalar
    MAX, MIN, ADD, MUL = AluOpType.max, AluOpType.min, AluOpType.add, AluOpType.mult
    X = AxisListType.X
    chip_a, chip_b = _chips(T, topo)

    if T.rank_of(core) is None:
        for here, there in ((chip_a, chip_b), (chip_b, chip_a)):
            _, _, partner, helper = _plan(topo, here, there)
            for c in here:
                if helper.get(c) == core:
                    mk = topo.mask(core, partner[c])
                    rid, pid = topo.addr(partner[c], core)
                    g.wait_ge(S.wn, _bits(topo.mask(c, core)))
                    g.remote_dma(out_ap=T.wp_sb[:, :], in_ap=T.wn_sb[:, :], remote_sem=S.wp, local_sem=S.snt, pid=pid,
                                 routing_id=rid, dma_engine_mask=mk)
                    g.wait_ge(S.snt, _bits(mk))
        return

    mine, other = (chip_a, chip_b) if core in chip_a else (chip_b, chip_a)
    owners, owner_of, partner, helper = _plan(topo, mine, other)
    owners_o, owner_of_o, partner_o, helper_o = _plan(topo, other, mine)
    is_owner = core in owners
    slot = mine.index(core)
    m_slot = slice(4 * slot, 4 * slot + 4)
    s_slot = slice(8 * slot, 8 * slot + 8)
    peers = [c for c in mine if c != core]
    m_on = topo.mask(core, peers[0])
    wsrc = [c for c in other if partner_o[c] == core][0]
    n_wp = _bits(topo.mask(wsrc if wsrc in owners_o else helper_o[wsrc], core))
    n_cmr = _bits(topo.mask(wsrc if wsrc in owners_o else owner_of_o[wsrc], core))
    ZA = [T["ZA%d" % b] for b in range(4)]
    ZB = [T["ZB%d" % b] for b in range(4)]

    def did(d):
        rid, pid = topo.addr(d, core)
        return DstId(rid=rid, pnc=pid)

    def piece_mask(c, d):
        on = topo.mask(c, d)
        if c not in owners:
            return on
        off = topo.mask(c, partner[c])
        return (on & off) if d in owners else (on & ~off)

    def copy_to(dsts, buf, cols, mask, sem):
        return RemoteDMATransfer(dst_ids=[did(c) for c in dsts], dma_engine_mask=mask, remote_sem=sem,
                                 srcs=[buf[:, cols]], dsts=[buf[:, cols] for c in dsts], alu_op=0)

    n_ma = sum(_bits(piece_mask(c, core)) for c in peers)

    g.sync.dma_start(T.h_sb[:, :], T.h[:, :]).then_inc(S.lh, 16)
    ACT.dma_start(T.w_sb[:, :], T.w[:, :]).then_inc(S.lw, 16)

    PE.wait_ge(S.lh, 16)
    PE.wait_ge(S.lw, 16)
    for b in range(4):
        PE.matmul(ZA[b][:, 0:128], T.h_sb[:, b:512:4], T.w_sb[:, :], True, True).then_inc(S["pa%d" % b], 1)
    PE.wait_ge(S.wp, n_wp)
    for b in (2, 3, 0, 1):
        PE.matmul(ZB[b][:, 0:128], T.h_sb[:, b:512:4], T.wp_sb[:, :], True, True).then_inc(S["pb%d" % b], 1)

    for b in range(4):
        V.wait_ge(S["pa%d" % b], 1)
        V.tensor_reduce(T.land_m[:, 4 * slot + b:4 * slot + b + 1], ZA[b][:, 0:128], X, MAX).then_inc(S.red, 1)

    sent = 0
    g.wait_ge(S.lw, 16)
    if is_owner:
        m_off = topo.mask(core, partner[core])
        rid, pid = topo.addr(partner[core], core)
        g.remote_dma(out_ap=T.wp_sb[:, :], in_ap=T.w_sb[:, :], remote_sem=S.wp, local_sem=S.snt, pid=pid, routing_id=rid,
                     dma_engine_mask=m_off)
        sent += _bits(m_off)
        g.wait_ge(S.red, 4)
        to_o = [c for c in owners if c != core]
        to_n = [c for c in peers if c not in owners]
        g.remote_dma_fused([copy_to(to_o, T.land_m, m_slot, piece_mask(core, to_o[0]), S.ma),
                            copy_to(to_n, T.land_m, m_slot, piece_mask(core, to_n[0]), S.ma)], local_sem=S.snt)
        sent += _bits(piece_mask(core, to_o[0])) + _bits(piece_mask(core, to_n[0]))
        g.wait_ge(S.ma, n_ma)
        far = [partner[core]] + [partner[c] for c in mine if owner_of.get(c) == core]
        g.remote_dma_fused([RemoteDMATransfer(dst_ids=[did(c) for c in far], dma_engine_mask=m_off, remote_sem=S.cmr,
                                              srcs=[T.land_m[:, 4 * k:4 * k + 4] for k in range(len(mine))],
                                              dsts=[T.cm_rem[:, :] for c in far], alu_op=2)], local_sem=S.snt)
        sent += _bits(m_off)
    else:
        hp = helper[core]
        m_hp = topo.mask(core, hp)
        rid, pid = topo.addr(hp, core)
        g.remote_dma(out_ap=T.wn_sb[:, :], in_ap=T.w_sb[:, :], remote_sem=S.wn, local_sem=S.snt, pid=pid, routing_id=rid,
                     dma_engine_mask=m_hp)
        sent += _bits(m_hp)
        g.wait_ge(S.red, 4)
        g.remote_dma_fused([copy_to(owners, T.land_m, m_slot, m_on, S.ma)], local_sem=S.snt)
        g.remote_dma_fused([copy_to([c for c in peers if c not in owners], T.land_m, m_slot, m_on, S.ma)], local_sem=S.snt)
        sent += 2 * _bits(m_on)

    V.wait_ge(S.red, 4)
    V.wait_ge(S.ma, n_ma)
    V.tensor_tensor(T.G1[:, :], T.land_m[:, 0:16], T.land_m[:, 16:32], MAX).then_inc(S.g1, 1)
    V.wait_ge(S.g1, 1)
    V.tensor_tensor(T.G2[:, :], T.G1[:, 0:8], T.G1[:, 8:16], MAX).then_inc(S.g2, 1)
    V.wait_ge(S.g2, 1)
    V.tensor_tensor(T.G3[:, :], T.G2[:, 0:4], T.G2[:, 4:8], MAX).then_inc(S.g3, 1)
    V.wait_ge(S.g3, 1)
    V.tensor_scalar(T.G3h[:, :], T.G3[:, :], -0.5, None, MUL).then_inc(S.g3h, 1)
    V.wait_ge(S.g3h, 1)
    V.wait_ge(S.cmr, n_cmr)
    for b in range(4):
        V.tensor_scalar(T.nb[:, b:b + 1], T.cm_rem[:, b:b + 1], -0.5, T.G3h[:, b:b + 1], MUL, MIN).then_inc(S["nb%d" % b], 1)
    V.tensor_tensor(T.m4[:, :], T.G3[:, :], T.cm_rem[:, :], MAX).then_inc(S.mm, 1)
    g.sync.wait_ge(S.mm, 1)
    g.sync.dma_start(T.m[:, :], T.m4[:, :]).then_inc(S.stm, 16)

    for k in range(6):
        b = k % 4
        ACT.wait_ge(S["nb%d" % b] if k < 4 else S["pb%d" % b], 1)
        ACT.activation(T.RS[:, 128 * k:128 * k + 128], (ZA if k < 4 else ZB)[b][:, 0:128], ActivationFunctionType.Relu,
                       bias=T.nb[:, b:b + 1], scale=1.0,
                       accum_out=T.land_s[:, 8 * slot + k:8 * slot + k + 1]).then_inc(S.act, 1)
    for b in (2, 3):
        V.wait_ge(S["nb%d" % b], 1)
        V.wait_ge(S["pb%d" % b], 1)
        V.tensor_scalar(T.RV[:, 128 * (b - 2):128 * (b - 1)], ZB[b][:, 0:128], T.nb[:, b:b + 1], 0.0, ADD, MAX).then_inc(S.rv, 1)
    V.wait_ge(S.rv, 2)
    for b in (2, 3):
        V.tensor_reduce(T.land_s[:, 8 * slot + 4 + b:8 * slot + 5 + b], T.RV[:, 128 * (b - 2):128 * (b - 1)], X,
                        ADD).then_inc(S.rr, 1)

    g.wait_ge(S.act, 6)
    g.wait_ge(S.rr, 2)
    g.remote_dma_fused([copy_to(peers, T.land_s, s_slot, m_on, S.sa)], local_sem=S.snt)
    sent += _bits(m_on)

    n_sa = sum(_bits(topo.mask(c, core)) for c in peers)
    V.wait_ge(S.rr, 2)
    V.wait_ge(S.act, 6)
    V.wait_ge(S.sa, n_sa)
    for b in (0, 1):
        V.tensor_reduce(T.s4[:, b:b + 1], T.land_s[:, b:64:4], X, ADD).then_inc(S.fv, 1)
    ACT.wait_ge(S.act, 6)
    ACT.wait_ge(S.rr, 2)
    ACT.wait_ge(S.sa, n_sa)
    for b in (2, 3):
        ACT.activation(T.J[:, 16 * (b - 2):16 * (b - 1)], T.land_s[:, b:64:4], ActivationFunctionType.Identity,
                       accum_out=T.s4[:, b:b + 1]).then_inc(S.fa, 1)
    g.sync.wait_ge(S.fv, 2)
    g.sync.wait_ge(S.fa, 2)
    g.sync.dma_start(T.s[:, :], T.s4[:, :]).then_inc(S.sts, 16)
    g.wait_ge(S.snt, sent)
    g.wait_ge(S.stm, 16)
    g.wait_ge(S.sts, 16)
